import numpy as np, ml_dtypes
CORES = [32,33,40,41,48,49,56,57,64,65,72,73]
N = 12
T = 8
ROUTE = [[[3,0],[2,5],[5,11],[7,1],[5,7],[7,8],[7,2],[2,4]],[[0,7],[2,11],[11,2],[5,4],[9,5],[5,1],[10,0],[0,10]],[[9,10],[10,6],[1,9],[3,2],[2,3],[2,6],[6,4],[1,9]],[[3,10],[0,9],[11,9],[11,9],[10,3],[6,1],[6,9],[8,7]],[[7,1],[0,4],[7,0],[5,3],[9,11],[8,10],[3,4],[8,2]],[[9,11],[3,1],[6,5],[10,3],[5,7],[4,10],[9,5],[7,0]],[[7,10],[4,2],[5,11],[2,1],[0,10],[2,11],[8,10],[11,4]],[[3,0],[5,4],[2,10],[10,9],[3,9],[8,6],[4,9],[4,0]],[[0,10],[4,8],[6,4],[2,1],[4,7],[9,7],[10,5],[4,10]],[[10,6],[1,8],[6,11],[9,8],[5,10],[11,5],[11,1],[3,11]],[[1,4],[6,3],[5,1],[9,7],[0,6],[9,5],[0,4],[3,5]],[[0,1],[11,4],[7,6],[8,1],[3,5],[6,11],[7,4],[7,9]]]
ZW = 19
def setup_inputs(rng):
    return {"z": rng.standard_normal((N, 128, ZW), dtype=np.float32).astype(ml_dtypes.bfloat16)}
def reference(z):
    y = np.zeros((N, 128, T), np.float64)
    fill = [0] * N
    for r in range(N):
        for t in range(T):
            for e in ROUTE[r][t]:
                y[r][:, t] += z[e][:, fill[e]].astype(np.float64)
                fill[e] += 1
    return {"y": y.astype(z.dtype)}

@@ -1,0 +1,148 @@
+from concourse.bass import DstId, RemoteDMATransfer
+from concourse.mybir import AluOpType
+
+SCRATCH = {
+    "zs": ("sbuf", [128, 19], "bfloat16"),
+    "land": ("sbuf", [128, 16], "bfloat16"),
+    "kin": ("sbuf", [128, 16], "bfloat16"),
+}
+SEMAPHORES = ["ld", "loc", "acc", "st", "arr", "karr", "sent"]
+
+
+def bits(m):
+    return bin(m).count("1")
+
+
+def make_plan(T, topo):
+    cores = T.cores
+    route = T.tables["ROUTE"]
+    n, nt = len(cores), len(route[0])
+    par = [topo.chip(c) & 1 for c in cores]
+    fill = [0] * n
+    direct = [[] for _ in range(n)]
+    kcols = [dict() for _ in range(n)]
+    ktok = [[] for _ in range(n)]
+    adds = [[] for _ in range(n)]
+    for r in range(n):
+        for t in range(nt):
+            same, cross = [], []
+            for e in route[r][t]:
+                (same if par[e] == par[r] else cross).append((e, fill[e]))
+                fill[e] += 1
+            for e, k in cross:
+                kcols[r].setdefault(e, []).append(k)
+            if cross:
+                ktok[r].append((t, cross))
+                slots = [nt + t]
+            else:
+                slots = [t, nt + t]
+            for (e, k), pos in zip(same, slots):
+                direct[e].append((r, k, pos))
+            if same:
+                adds[r].append(t)
+    koff = [dict() for _ in range(n)]
+    for r in range(n):
+        o = 0
+        for e in sorted(kcols[r]):
+            koff[r][e] = o
+            o += len(kcols[r][e])
+    return dict(n=n, nt=nt, par=par, direct=direct, kcols=kcols, ktok=ktok, adds=adds, koff=koff)
+
+
+def combiner(topo, c):
+    return (topo.chip(c) ^ 1) * 8 + (2 if c % 8 == 0 else 6)
+
+
+def merged(items):
+    out = []
+    for r, k, pos in sorted(items, key=lambda x: x[1]):
+        if out and out[-1][0] == r and out[-1][1] + out[-1][3] == k and out[-1][2] + out[-1][3] == pos:
+            out[-1][3] += 1
+        else:
+            out.append([r, k, pos, 1])
+    return out
+
+
+def runs(ts):
+    out = []
+    for t in ts:
+        if out and out[-1][1] == t:
+            out[-1][1] = t + 1
+        else:
+            out.append([t, t + 1])
+    return out
+
+
+def rank_program(g, core, T, topo):
+    P = make_plan(T, topo)
+    cores, nt = T.cores, P["nt"]
+    rank = T.rank_of(core)
+
+    if rank is None:
+        served = [r for r in range(P["n"]) if combiner(topo, cores[r]) == core]
+        if not served:
+            return
+        r = served[0]
+        dst = cores[r]
+        need = sum(bits(topo.mask(cores[e], core)) for e in P["kcols"][r])
+        g.wait_ge(T.sem.karr, need)
+        rid, pid, _ = topo.addr(dst)
+        sent = 0
+        toks = P["ktok"][r]
+        for alu in (1, 0):
+            sel = [x for x in toks if (len(x[1]) > 1) == (alu == 1)]
+            for i in range(0, len(sel), 8):
+                trs = []
+                for j, (t, cs) in enumerate(sel[i:i + 8]):
+                    srcs = []
+                    for e, k in cs:
+                        p = P["koff"][r][e] + k - P["kcols"][r][e][0]
+                        srcs.append(T.kin[:, p:p + 1])
+                    trs.append(RemoteDMATransfer(dst_ids=[DstId(rid=rid, pnc=pid)], dma_engine_mask=1 << j,
+                                                 remote_sem=T.sem.arr, srcs=srcs, dsts=[T.land[:, t:t + 1]],
+                                                 alu_op=alu))
+                    sent += 1
+                g.remote_dma_fused(trs, local_sem=T.sem.sent)
+        g.wait_ge(T.sem.sent, sent)
+        return
+
+    e = rank
+    g.dma_start(T.zs[:], T.z[:]).then_inc(T.sem.ld, 16)
+    g.wait_ge(T.sem.ld, 16)
+    sent = 0
+    for r in range(P["n"]):
+        if e in P["kcols"][r]:
+            ks = P["kcols"][r][e]
+            o = P["koff"][r][e]
+            k_core = combiner(topo, cores[r])
+            rid, pid, _ = topo.addr(k_core)
+            m = topo.mask(core, k_core)
+            g.remote_dma(T.kin[:, o:o + len(ks)], T.zs[:, ks[0]:ks[0] + len(ks)], T.sem.karr, T.sem.sent,
+                         pid, rid, m)
+            sent += bits(m)
+    nloc = 0
+    for r, k, pos, w in merged(P["direct"][e]):
+        if r == e:
+            g.dma_start(T.land[:, pos:pos + w], T.zs[:, k:k + w]).then_inc(T.sem.loc, 16)
+            nloc += 16
+        else:
+            rid, pid, _ = topo.addr(cores[r])
+            m = topo.mask(core, cores[r])
+            g.remote_dma(T.land[:, pos:pos + w], T.zs[:, k:k + w], T.sem.arr, T.sem.sent, pid, rid, m)
+            sent += bits(m)
+    need = len(P["ktok"][e])
+    for s in range(P["n"]):
+        if s != e:
+            need += sum(bits(topo.mask(cores[s], core)) for x in merged(P["direct"][s]) if x[0] == e)
+    if nloc:
+        g.wait_ge(T.sem.loc, nloc)
+    g.wait_ge(T.sem.arr, need)
+    nacc = 0
+    for a, b in runs(P["adds"][e]):
+        g.dma_start(T.land[:, a:b], T.land[:, nt + a:nt + b], accum_op=AluOpType.add).then_inc(T.sem.acc, 16)
+        nacc += 16
+    if nacc:
+        g.wait_ge(T.sem.acc, nacc)
+    g.dma_start(T.y[:], T.land[:, 0:nt]).then_inc(T.sem.st, 16)
+    g.wait_ge(T.sem.st, 16)
+    g.wait_ge(T.sem.sent, sent)

@@ -1,66 +1,19 @@
 from concourse.bass import DstId, RemoteDMATransfer
 from concourse.mybir import AluOpType
 
+ZW_MAX = 19
+N_FOREIGN = 8
 SCRATCH = {
-    "zs": ("sbuf", [128, 19], "bfloat16"),
+    "zs": ("sbuf", [128, ZW_MAX], "bfloat16"),
     "land": ("sbuf", [128, 16], "bfloat16"),
-    "kin": ("sbuf", [128, 16], "bfloat16"),
+    "kin": ("sbuf", [128, 2 * ZW_MAX + N_FOREIGN], "bfloat16"),
 }
-SEMAPHORES = ["ld", "loc", "acc", "st", "arr", "karr", "sent"]
+SEMAPHORES = ["ld", "selfp", "selfq", "arrp", "arrq", "kloc", "kfor", "sent", "cpg", "cps", "fing", "fins"]
+PLAN = {}
 
 
 def bits(m):
     return bin(m).count("1")
-
-
-def make_plan(T, topo):
-    cores = T.cores
-    route = T.tables["ROUTE"]
-    n, nt = len(cores), len(route[0])
-    par = [topo.chip(c) & 1 for c in cores]
-    fill = [0] * n
-    direct = [[] for _ in range(n)]
-    kcols = [dict() for _ in range(n)]
-    ktok = [[] for _ in range(n)]
-    adds = [[] for _ in range(n)]
-    for r in range(n):
-        for t in range(nt):
-            same, cross = [], []
-            for e in route[r][t]:
-                (same if par[e] == par[r] else cross).append((e, fill[e]))
-                fill[e] += 1
-            for e, k in cross:
-                kcols[r].setdefault(e, []).append(k)
-            if cross:
-                ktok[r].append((t, cross))
-                slots = [nt + t]
-            else:
-                slots = [t, nt + t]
-            for (e, k), pos in zip(same, slots):
-                direct[e].append((r, k, pos))
-            if same:
-                adds[r].append(t)
-    koff = [dict() for _ in range(n)]
-    for r in range(n):
-        o = 0
-        for e in sorted(kcols[r]):
-            koff[r][e] = o
-            o += len(kcols[r][e])
-    return dict(n=n, nt=nt, par=par, direct=direct, kcols=kcols, ktok=ktok, adds=adds, koff=koff)
-
-
-def combiner(topo, c):
-    return (topo.chip(c) ^ 1) * 8 + (2 if c % 8 == 0 else 6)
-
-
-def merged(items):
-    out = []
-    for r, k, pos in sorted(items, key=lambda x: x[1]):
-        if out and out[-1][0] == r and out[-1][1] + out[-1][3] == k and out[-1][2] + out[-1][3] == pos:
-            out[-1][3] += 1
-        else:
-            out.append([r, k, pos, 1])
-    return out
 
 
 def runs(ts):
@@ -73,76 +26,237 @@ def runs(ts):
     return out
 
 
-def rank_program(g, core, T, topo):
-    P = make_plan(T, topo)
-    cores, nt = T.cores, P["nt"]
-    rank = T.rank_of(core)
+def make_plan(cores, route):
+    n, nt = len(cores), len(route[0])
+    chip = [c // 8 for c in cores]
+    par = [c & 1 for c in chip]
+    pairs = sorted(set(c // 2 for c in chip))
 
-    if rank is None:
-        served = [r for r in range(P["n"]) if combiner(topo, cores[r]) == core]
-        if not served:
-            return
-        r = served[0]
-        dst = cores[r]
-        need = sum(bits(topo.mask(cores[e], core)) for e in P["kcols"][r])
-        g.wait_ge(T.sem.karr, need)
-        rid, pid, _ = topo.addr(dst)
-        sent = 0
-        toks = P["ktok"][r]
-        for alu in (1, 0):
-            sel = [x for x in toks if (len(x[1]) > 1) == (alu == 1)]
-            for i in range(0, len(sel), 8):
-                trs = []
-                for j, (t, cs) in enumerate(sel[i:i + 8]):
-                    srcs = []
-                    for e, k in cs:
-                        p = P["koff"][r][e] + k - P["kcols"][r][e][0]
-                        srcs.append(T.kin[:, p:p + 1])
-                    trs.append(RemoteDMATransfer(dst_ids=[DstId(rid=rid, pnc=pid)], dma_engine_mask=1 << j,
-                                                 remote_sem=T.sem.arr, srcs=srcs, dsts=[T.land[:, t:t + 1]],
-                                                 alu_op=alu))
-                    sent += 1
-                g.remote_dma_fused(trs, local_sem=T.sem.sent)
-        g.wait_ge(T.sem.sent, sent)
-        return
+    def helper(d, r):
+        if chip[r] == d:
+            return d * 8 + (4 if cores[r] % 8 == 0 else 5)
+        if chip[r] == d ^ 1:
+            return d * 8 + (2 if cores[r] % 8 == 0 else 3)
+        others = [p for p in pairs if p != d // 2]
+        return d * 8 + (6 if others.index(chip[r] // 2) % 2 == (d // 2) % 2 else 7)
 
-    e = rank
-    g.dma_start(T.zs[:], T.z[:]).then_inc(T.sem.ld, 16)
-    g.wait_ge(T.sem.ld, 16)
-    sent = 0
-    for r in range(P["n"]):
-        if e in P["kcols"][r]:
-            ks = P["kcols"][r][e]
-            o = P["koff"][r][e]
-            k_core = combiner(topo, cores[r])
-            rid, pid, _ = topo.addr(k_core)
-            m = topo.mask(core, k_core)
-            g.remote_dma(T.kin[:, o:o + len(ks)], T.zs[:, ks[0]:ks[0] + len(ks)], T.sem.karr, T.sem.sent,
-                         pid, rid, m)
-            sent += bits(m)
-    nloc = 0
-    for r, k, pos, w in merged(P["direct"][e]):
-        if r == e:
-            g.dma_start(T.land[:, pos:pos + w], T.zs[:, k:k + w]).then_inc(T.sem.loc, 16)
-            nloc += 16
+    direct = [[] for _ in range(n)]
+    foreign = [[] for _ in range(n)]
+    hsend = {}
+    nfor = {}
+    load = [0] * n
+    has_p = [[] for _ in range(n)]
+
+    def by_helper(d, r, t, cs):
+        h = helper(d, r)
+        away = [x for x in cs if chip[x[0]] != d]
+        hsend.setdefault(h, []).append((r, t, cs, bool(away)))
+        for e, k in away:
+            foreign[e].append((h, k, nfor.get(h, 0)))
+            nfor[h] = nfor.get(h, 0) + 1
+            load[e] += 1
+
+    def straight(x, r, pos):
+        direct[x[0]].append((r, x[1], pos))
+        load[x[0]] += x[0] != r
+
+    fill = [0] * n
+    tok = {}
+    for r in range(n):
+        for t in range(nt):
+            same, other = [], []
+            for e in route[r][t]:
+                (same if par[e] == par[r] else other).append((e, fill[e]))
+                fill[e] += 1
+            tok[(r, t)] = (same, other)
+    folded = []
+    for r in range(n):
+        must = [t for t in range(nt) if len(tok[(r, t)][1]) == 2]
+        may = [t for t in range(nt) if len(tok[(r, t)][0]) == 2]
+        best = None
+        for m in range(1 << len(may)):
+            f = sorted(must + [t for i, t in enumerate(may) if m >> i & 1])
+            p = [t for t in range(nt) if t not in f]
+            own = [t for t in range(nt) if any(e == r for e, _k in tok[(r, t)][0])]
+            cost = (2 * len(runs(p)) + len(runs(f)) + len(runs([t for t in own if t in p]))
+                    + (1 if [t for t in own if t in f] else 0))
+            if best is None or (cost, len(f)) < best[0]:
+                best = ((cost, len(f)), f)
+        folded.append(best[1])
+        has_p[r] = [t for t in range(nt) if t not in best[1]]
+    later = []
+    for r in range(n):
+        for t in range(nt):
+            same, other = tok[(r, t)]
+            if len(other) == 1:
+                straight(same[0], r, t)
+                by_helper(chip[other[0][0]], r, t, other)
+            else:
+                later.append((r, t, same + other))
+    for r, t, cs in later:
+        if t in folded[r]:
+            a, b = cs
+            good = [chip[r], chip[r] ^ 1]
+            if chip[b[0]] in good and chip[a[0]] not in good:
+                a, b = b, a
+            elif chip[a[0]] not in good and load[a[0]] < load[b[0]]:
+                a, b = b, a
+            by_helper(chip[a[0]], r, t, [a, b])
         else:
+            a, b = sorted(cs, key=lambda x: (x[0] != r, chip[x[0]] != chip[r], load[x[0]]))
+            straight(a, r, t)
+            if chip[b[0]] == chip[r]:
+                straight(b, r, nt + t)
+            else:
+                by_helper(chip[b[0]], r, t, [b])
+    blocks = {}
+    for h in sorted(hsend):
+        for r, t, cs, _f in hsend[h]:
+            for e, k in cs:
+                if chip[e] == h // 8:
+                    b = blocks.setdefault((e, h), [k, k + 1])
+                    b[0], b[1] = min(b[0], k), max(b[1], k + 1)
+    return dict(n=n, nt=nt, chip=chip, direct=direct, foreign=foreign, hsend=hsend, has_p=has_p, blocks=blocks)
+
+
+def merged(items, nt):
+    out = []
+    for r, k, pos in sorted(items, key=lambda x: x[1]):
+        if (out and out[-1][0] == r and out[-1][1] + out[-1][3] == k and out[-1][2] + out[-1][3] == pos
+                and pos != nt):
+            out[-1][3] += 1
+        else:
+            out.append([r, k, pos, 1])
+    return out
+
+
+def helper_program(g, core, T, topo, P):
+    cores, nt, zw = T.cores, P["nt"], T.tables["ZW"]
+    fcol = {}
+    n_for = 0
+    for e in range(P["n"]):
+        for h, k, j in P["foreign"][e]:
+            if h == core:
+                fcol[(e, k)] = 2 * zw + j
+                n_for += bits(topo.mask(cores[e], core))
+
+    def col(e, k):
+        if P["chip"][e] == core // 8:
+            return (cores[e] % 8) * zw + k
+        return fcol[(e, k)]
+
+    sent = 0
+    g.wait_ge(T.sem.kloc, sum(bits(topo.mask(cores[e], core)) for (e, h) in P["blocks"] if h == core))
+    for phase in (False, True):
+        sel = [s for s in P["hsend"][core] if s[3] == phase]
+        if phase and sel:
+            g.wait_ge(T.sem.kfor, n_for)
+        for r, t, cs, _f in sel:
             rid, pid, _ = topo.addr(cores[r])
             m = topo.mask(core, cores[r])
-            g.remote_dma(T.land[:, pos:pos + w], T.zs[:, k:k + w], T.sem.arr, T.sem.sent, pid, rid, m)
+            srcs = [T.kin[:, col(e, k):col(e, k) + 1] for e, k in cs]
+            dst = T.land[:, nt + t:nt + t + 1]
+            if len(srcs) == 1:
+                g.remote_dma(dst, srcs[0], T.sem.arrq, T.sem.sent, pid, rid, m)
+            else:
+                g.remote_dma_fused([RemoteDMATransfer(dst_ids=[DstId(rid=rid, pnc=pid)], dma_engine_mask=m,
+                                                      remote_sem=T.sem.arrq, srcs=srcs, dsts=[dst], alu_op=1)],
+                                   local_sem=T.sem.sent)
             sent += bits(m)
-    need = len(P["ktok"][e])
-    for s in range(P["n"]):
-        if s != e:
-            need += sum(bits(topo.mask(cores[s], core)) for x in merged(P["direct"][s]) if x[0] == e)
-    if nloc:
-        g.wait_ge(T.sem.loc, nloc)
-    g.wait_ge(T.sem.arr, need)
-    nacc = 0
-    for a, b in runs(P["adds"][e]):
-        g.dma_start(T.land[:, a:b], T.land[:, nt + a:nt + b], accum_op=AluOpType.add).then_inc(T.sem.acc, 16)
-        nacc += 16
-    if nacc:
-        g.wait_ge(T.sem.acc, nacc)
-    g.dma_start(T.y[:], T.land[:, 0:nt]).then_inc(T.sem.st, 16)
-    g.wait_ge(T.sem.st, 16)
+    g.wait_ge(T.sem.sent, sent)
+
+
+def rank_program(g, core, T, topo):
+    if "p" not in PLAN:
+        PLAN["p"] = make_plan(T.cores, T.tables["ROUTE"])
+    P = PLAN["p"]
+    cores, nt, zw, n = T.cores, P["nt"], T.tables["ZW"], P["n"]
+    me = T.rank_of(core)
+    if me is None:
+        if core in P["hsend"]:
+            helper_program(g, core, T, topo, P)
+        return
+
+    g.sync.dma_start(T.zs[:, 0:zw], T.z[:]).then_inc(T.sem.ld, 16)
+    pieces = merged(P["direct"][me], nt)
+    own = [x for x in pieces if x[0] == me]
+    n_self = [0, 0]
+    if own:
+        g.sync.wait_ge(T.sem.ld, 16)
+    for _r, k, pos, w in own:
+        q = pos >= nt
+        g.sync.dma_start(T.land[:, pos:pos + w], T.zs[:, k:k + w]).then_inc(T.sem.selfq if q else T.sem.selfp, 16)
+        n_self[q] += 16
+
+    g.wait_ge(T.sem.ld, 16)
+    sent = 0
+    for h in sorted([h for (e, h) in P["blocks"] if e == me], key=lambda h: -len(P["hsend"][h])):
+        a, b = P["blocks"][(me, h)]
+        rid, pid, _ = topo.addr(h)
+        m = topo.mask(core, h)
+        o = (core % 8) * zw
+        g.remote_dma(T.kin[:, o + a:o + b], T.zs[:, a:b], T.sem.kloc, T.sem.sent, pid, rid, m)
+        sent += bits(m)
+    for h, k, j in P["foreign"][me]:
+        rid, pid, _ = topo.addr(h)
+        m = topo.mask(core, h)
+        g.remote_dma(T.kin[:, 2 * zw + j:2 * zw + j + 1], T.zs[:, k:k + 1], T.sem.kfor, T.sem.sent, pid, rid, m)
+        sent += bits(m)
+    for r, k, pos, w in sorted([x for x in pieces if x[0] != me], key=lambda x: x[2] >= nt):
+        rid, pid, _ = topo.addr(cores[r])
+        m = topo.mask(core, cores[r])
+        g.remote_dma(T.land[:, pos:pos + w], T.zs[:, k:k + w], T.sem.arrq if pos >= nt else T.sem.arrp,
+                     T.sem.sent, pid, rid, m)
+        sent += bits(m)
+
+    need = [0, 0]
+    for e in range(n):
+        if e != me:
+            for r, _k, pos, _w in merged(P["direct"][e], nt):
+                if r == me:
+                    need[pos >= nt] += bits(topo.mask(cores[e], core))
+    for h in P["hsend"]:
+        need[1] += sum(bits(topo.mask(h, core)) for s in P["hsend"][h] if s[0] == me)
+
+    p_runs = runs(P["has_p"][me])
+    f_runs = runs([t for t in range(nt) if t not in P["has_p"][me]])
+    wide = [x for x in p_runs if x[1] - x[0] > 1]
+    thin = [x for x in p_runs if x[1] - x[0] == 1]
+    for q in ([g.scalar] if wide else []) + [g]:
+        if need[0]:
+            q.wait_ge(T.sem.arrp, need[0])
+        if n_self[0]:
+            q.wait_ge(T.sem.selfp, n_self[0])
+    for a, b in wide:
+        g.scalar.dma_start(T.y[:, a:b], T.land[:, a:b]).then_inc(T.sem.cps, 16)
+    for a, b in thin:
+        g.dma_start(T.y[:, a:b], T.land[:, a:b], allow_slow_non_contiguous=True).then_inc(T.sem.cpg, 16)
+
+    f_wide = [x for x in f_runs if x[1] - x[0] > 1]
+    f_thin = [x for x in f_runs if x[1] - x[0] == 1]
+    if f_wide:
+        g.scalar.wait_ge(T.sem.arrq, need[1])
+    for a, b in f_wide:
+        g.scalar.dma_start(T.y[:, a:b], T.land[:, nt + a:nt + b]).then_inc(T.sem.fins, 16)
+    g.wait_ge(T.sem.arrq, need[1])
+    if n_self[1]:
+        g.wait_ge(T.sem.selfq, n_self[1])
+    nfin = 0
+    for a, b in f_thin:
+        g.dma_start(T.y[:, a:b], T.land[:, nt + a:nt + b], allow_slow_non_contiguous=True).then_inc(T.sem.fing, 16)
+        nfin += 16
+    if wide:
+        g.wait_ge(T.sem.cps, 16 * len(wide))
+    if thin:
+        g.wait_ge(T.sem.cpg, 16 * len(thin))
+    for a, b in p_runs:
+        if b - a > 1:
+            g.dma_start(T.y[:, a:b], T.land[:, nt + a:nt + b], accum_op=AluOpType.add).then_inc(T.sem.fing, 16)
+        else:
+            g.dma_start(T.y[:, a:b], T.land[:, nt + a:nt + b], accum_op=AluOpType.add,
+                        allow_slow_non_contiguous=True).then_inc(T.sem.fing, 16)
+        nfin += 16
+    g.wait_ge(T.sem.fing, nfin)
+    if f_wide:
+        g.wait_ge(T.sem.fins, 16 * len(f_wide))
     g.wait_ge(T.sem.sent, sent)

from concourse.bass import DstId, RemoteDMATransfer
from concourse.mybir import AluOpType

ZW_MAX = 19
N_FOREIGN = 8
SCRATCH = {
    "zs": ("sbuf", [128, ZW_MAX], "bfloat16"),
    "land": ("sbuf", [128, 16], "bfloat16"),
    "kin": ("sbuf", [128, 2 * ZW_MAX + N_FOREIGN], "bfloat16"),
}
SEMAPHORES = ["ld", "selfp", "selfq", "arrp", "arrq", "kloc", "kfor", "sent", "cpg", "cps", "fing", "fins"]
PLAN = {}


def bits(m):
    return bin(m).count("1")


def runs(ts):
    out = []
    for t in ts:
        if out and out[-1][1] == t:
            out[-1][1] = t + 1
        else:
            out.append([t, t + 1])
    return out


def make_plan(cores, route):
    n, nt = len(cores), len(route[0])
    chip = [c // 8 for c in cores]
    par = [c & 1 for c in chip]
    pairs = sorted(set(c // 2 for c in chip))

    def helper(d, r):
        if chip[r] == d:
            return d * 8 + (4 if cores[r] % 8 == 0 else 5)
        if chip[r] == d ^ 1:
            return d * 8 + (2 if cores[r] % 8 == 0 else 3)
        others = [p for p in pairs if p != d // 2]
        return d * 8 + (6 if others.index(chip[r] // 2) % 2 == (d // 2) % 2 else 7)

    direct = [[] for _ in range(n)]
    foreign = [[] for _ in range(n)]
    hsend = {}
    nfor = {}
    load = [0] * n
    has_p = [[] for _ in range(n)]

    def by_helper(d, r, t, cs):
        h = helper(d, r)
        away = [x for x in cs if chip[x[0]] != d]
        hsend.setdefault(h, []).append((r, t, cs, bool(away)))
        for e, k in away:
            foreign[e].append((h, k, nfor.get(h, 0)))
            nfor[h] = nfor.get(h, 0) + 1
            load[e] += 1

    def straight(x, r, pos):
        direct[x[0]].append((r, x[1], pos))
        load[x[0]] += x[0] != r

    fill = [0] * n
    tok = {}
    for r in range(n):
        for t in range(nt):
            same, other = [], []
            for e in route[r][t]:
                (same if par[e] == par[r] else other).append((e, fill[e]))
                fill[e] += 1
            tok[(r, t)] = (same, other)
    folded = []
    for r in range(n):
        must = [t for t in range(nt) if len(tok[(r, t)][1]) == 2]
        may = [t for t in range(nt) if len(tok[(r, t)][0]) == 2]
        best = None
        for m in range(1 << len(may)):
            f = sorted(must + [t for i, t in enumerate(may) if m >> i & 1])
            p = [t for t in range(nt) if t not in f]
            own = [t for t in range(nt) if any(e == r for e, _k in tok[(r, t)][0])]
            cost = (2 * len(runs(p)) + len(runs(f)) + len(runs([t for t in own if t in p]))
                    + (1 if [t for t in own if t in f] else 0))
            if best is None or (cost, len(f)) < best[0]:
                best = ((cost, len(f)), f)
        folded.append(best[1])
        has_p[r] = [t for t in range(nt) if t not in best[1]]
    later = []
    for r in range(n):
        for t in range(nt):
            same, other = tok[(r, t)]
            if len(other) == 1:
                straight(same[0], r, t)
                by_helper(chip[other[0][0]], r, t, other)
            else:
                later.append((r, t, same + other))
    for r, t, cs in later:
        if t in folded[r]:
            a, b = cs
            good = [chip[r], chip[r] ^ 1]
            if chip[b[0]] in good and chip[a[0]] not in good:
                a, b = b, a
            elif chip[a[0]] not in good and load[a[0]] < load[b[0]]:
                a, b = b, a
            by_helper(chip[a[0]], r, t, [a, b])
        else:
            a, b = sorted(cs, key=lambda x: (x[0] != r, chip[x[0]] != chip[r], load[x[0]]))
            straight(a, r, t)
            if chip[b[0]] == chip[r]:
                straight(b, r, nt + t)
            else:
                by_helper(chip[b[0]], r, t, [b])
    blocks = {}
    for h in sorted(hsend):
        for r, t, cs, _f in hsend[h]:
            for e, k in cs:
                if chip[e] == h // 8:
                    b = blocks.setdefault((e, h), [k, k + 1])
                    b[0], b[1] = min(b[0], k), max(b[1], k + 1)
    return dict(n=n, nt=nt, chip=chip, direct=direct, foreign=foreign, hsend=hsend, has_p=has_p, blocks=blocks)


def merged(items, nt):
    out = []
    for r, k, pos in sorted(items, key=lambda x: x[1]):
        if (out and out[-1][0] == r and out[-1][1] + out[-1][3] == k and out[-1][2] + out[-1][3] == pos
                and pos != nt):
            out[-1][3] += 1
        else:
            out.append([r, k, pos, 1])
    return out


def helper_program(g, core, T, topo, P):
    cores, nt, zw = T.cores, P["nt"], T.tables["ZW"]
    fcol = {}
    n_for = 0
    for e in range(P["n"]):
        for h, k, j in P["foreign"][e]:
            if h == core:
                fcol[(e, k)] = 2 * zw + j
                n_for += bits(topo.mask(cores[e], core))

    def col(e, k):
        if P["chip"][e] == core // 8:
            return (cores[e] % 8) * zw + k
        return fcol[(e, k)]

    sent = 0
    g.wait_ge(T.sem.kloc, sum(bits(topo.mask(cores[e], core)) for (e, h) in P["blocks"] if h == core))
    for phase in (False, True):
        sel = [s for s in P["hsend"][core] if s[3] == phase]
        if phase and sel:
            g.wait_ge(T.sem.kfor, n_for)
        for r, t, cs, _f in sel:
            rid, pid, _ = topo.addr(cores[r])
            m = topo.mask(core, cores[r])
            srcs = [T.kin[:, col(e, k):col(e, k) + 1] for e, k in cs]
            dst = T.land[:, nt + t:nt + t + 1]
            if len(srcs) == 1:
                g.remote_dma(dst, srcs[0], T.sem.arrq, T.sem.sent, pid, rid, m)
            else:
                g.remote_dma_fused([RemoteDMATransfer(dst_ids=[DstId(rid=rid, pnc=pid)], dma_engine_mask=m,
                                                      remote_sem=T.sem.arrq, srcs=srcs, dsts=[dst], alu_op=1)],
                                   local_sem=T.sem.sent)
            sent += bits(m)
    g.wait_ge(T.sem.sent, sent)


def rank_program(g, core, T, topo):
    if "p" not in PLAN:
        PLAN["p"] = make_plan(T.cores, T.tables["ROUTE"])
    P = PLAN["p"]
    cores, nt, zw, n = T.cores, P["nt"], T.tables["ZW"], P["n"]
    me = T.rank_of(core)
    if me is None:
        if core in P["hsend"]:
            helper_program(g, core, T, topo, P)
        return

    g.sync.dma_start(T.zs[:, 0:zw], T.z[:]).then_inc(T.sem.ld, 16)
    pieces = merged(P["direct"][me], nt)
    own = [x for x in pieces if x[0] == me]
    n_self = [0, 0]
    if own:
        g.sync.wait_ge(T.sem.ld, 16)
    for _r, k, pos, w in own:
        q = pos >= nt
        g.sync.dma_start(T.land[:, pos:pos + w], T.zs[:, k:k + w]).then_inc(T.sem.selfq if q else T.sem.selfp, 16)
        n_self[q] += 16

    g.wait_ge(T.sem.ld, 16)
    sent = 0
    for h in sorted([h for (e, h) in P["blocks"] if e == me], key=lambda h: -len(P["hsend"][h])):
        a, b = P["blocks"][(me, h)]
        rid, pid, _ = topo.addr(h)
        m = topo.mask(core, h)
        o = (core % 8) * zw
        g.remote_dma(T.kin[:, o + a:o + b], T.zs[:, a:b], T.sem.kloc, T.sem.sent, pid, rid, m)
        sent += bits(m)
    for h, k, j in P["foreign"][me]:
        rid, pid, _ = topo.addr(h)
        m = topo.mask(core, h)
        g.remote_dma(T.kin[:, 2 * zw + j:2 * zw + j + 1], T.zs[:, k:k + 1], T.sem.kfor, T.sem.sent, pid, rid, m)
        sent += bits(m)
    for r, k, pos, w in sorted([x for x in pieces if x[0] != me], key=lambda x: x[2] >= nt):
        rid, pid, _ = topo.addr(cores[r])
        m = topo.mask(core, cores[r])
        g.remote_dma(T.land[:, pos:pos + w], T.zs[:, k:k + w], T.sem.arrq if pos >= nt else T.sem.arrp,
                     T.sem.sent, pid, rid, m)
        sent += bits(m)

    need = [0, 0]
    for e in range(n):
        if e != me:
            for r, _k, pos, _w in merged(P["direct"][e], nt):
                if r == me:
                    need[pos >= nt] += bits(topo.mask(cores[e], core))
    for h in P["hsend"]:
        need[1] += sum(bits(topo.mask(h, core)) for s in P["hsend"][h] if s[0] == me)

    p_runs = runs(P["has_p"][me])
    f_runs = runs([t for t in range(nt) if t not in P["has_p"][me]])
    wide = [x for x in p_runs if x[1] - x[0] > 1]
    thin = [x for x in p_runs if x[1] - x[0] == 1]
    for q in ([g.scalar] if wide else []) + [g]:
        if need[0]:
            q.wait_ge(T.sem.arrp, need[0])
        if n_self[0]:
            q.wait_ge(T.sem.selfp, n_self[0])
    for a, b in wide:
        g.scalar.dma_start(T.y[:, a:b], T.land[:, a:b]).then_inc(T.sem.cps, 16)
    for a, b in thin:
        g.dma_start(T.y[:, a:b], T.land[:, a:b], allow_slow_non_contiguous=True).then_inc(T.sem.cpg, 16)

    f_wide = [x for x in f_runs if x[1] - x[0] > 1]
    f_thin = [x for x in f_runs if x[1] - x[0] == 1]
    if f_wide:
        g.scalar.wait_ge(T.sem.arrq, need[1])
    for a, b in f_wide:
        g.scalar.dma_start(T.y[:, a:b], T.land[:, nt + a:nt + b]).then_inc(T.sem.fins, 16)
    g.wait_ge(T.sem.arrq, need[1])
    if n_self[1]:
        g.wait_ge(T.sem.selfq, n_self[1])
    nfin = 0
    for a, b in f_thin:
        g.dma_start(T.y[:, a:b], T.land[:, nt + a:nt + b], allow_slow_non_contiguous=True).then_inc(T.sem.fing, 16)
        nfin += 16
    if wide:
        g.wait_ge(T.sem.cps, 16 * len(wide))
    if thin:
        g.wait_ge(T.sem.cpg, 16 * len(thin))
    for a, b in p_runs:
        if b - a > 1:
            g.dma_start(T.y[:, a:b], T.land[:, nt + a:nt + b], accum_op=AluOpType.add).then_inc(T.sem.fing, 16)
        else:
            g.dma_start(T.y[:, a:b], T.land[:, nt + a:nt + b], accum_op=AluOpType.add,
                        allow_slow_non_contiguous=True).then_inc(T.sem.fing, 16)
        nfin += 16
    g.wait_ge(T.sem.fing, nfin)
    if f_wide:
        g.wait_ge(T.sem.fins, 16 * len(f_wide))
    g.wait_ge(T.sem.sent, sent)
